import numpy as np
import ml_dtypes


def mxq(x, axis, fmt="e4m3"):
    dtype, down = {"e4m3": (ml_dtypes.float8_e4m3fn, 7), "e5m2": (ml_dtypes.float8_e5m2, 14)}[fmt]
    v = np.moveaxis(np.asarray(x, np.float32).astype(ml_dtypes.bfloat16).astype(np.float64), axis, -1)
    blocks = v.reshape(v.shape[:-1] + (-1, 32))
    amax = np.abs(blocks).max(-1, keepdims=True)
    byte = np.maximum(np.where(amax > 0, np.frexp(amax)[1] - 1 + 127, 0) - down, 1)
    scale = np.exp2(byte - 127.0)
    codes = (blocks / scale).astype(np.float32).astype(dtype).astype(np.float64)
    return np.moveaxis((codes * scale).reshape(v.shape), -1, axis)


WIDE = False


def mx_kscale(k):
    if not WIDE:
        return np.ones(k)
    levels = np.array([10, -10, 5, -5, 0])
    if k % 512:
        return np.exp2(np.random.permutation(np.resize(levels, k // 32))).repeat(32)
    a = np.empty((k // 512, 16))
    for p in range(k // 512):
        a[p, :8] = np.random.permutation(np.resize(levels, 8))
        for g in range(8):
            far = levels[np.abs(levels - a[p, g]) >= 10]
            a[p, g + 8] = far[np.random.randint(len(far))]
    return np.exp2(a.ravel()).repeat(32)


def f64(x):
    return np.asarray(x).astype(np.float64)


def striped(idx):
    return np.tile(idx.reshape(-1, 16).T, (8, 1)).astype(np.uint16)


def unstriped(offs):
    return offs[:16].T.reshape(-1).astype(np.int64)


E2M1 = np.array([0.0, 0.5, 1.0, 1.5, 2.0, 3.0, 4.0, 6.0, -0.0, -0.5, -1.0, -1.5, -2.0, -3.0, -4.0, -6.0])


def pack_weight(w, fmt):
    k, n = w.shape
    w = f64(np.asarray(w, np.float32).astype(ml_dtypes.bfloat16)).reshape(k // 32, 32, n)
    amax = np.abs(w).max(1)
    if fmt == "e4m3":
        byte = np.frexp(amax)[1] - 1 + 127 - 7
    else:
        mant, ex = np.frexp(amax / 6.0)
        byte = np.where(mant > 0.5, ex, ex - 1) + 127
    byte = np.clip(np.where(amax > 0, byte, 1), 1, 254)
    scaled = (w * np.exp2(127.0 - byte)[:, None, :]).reshape(k, n).astype(np.float32)
    by_word = np.ascontiguousarray(scaled.reshape(k // 512, 128, 4, n).transpose(0, 1, 3, 2))
    if fmt == "e4m3":
        words = by_word.astype(ml_dtypes.float8_e4m3fn).view(np.uint8)
    else:
        c = by_word.astype(ml_dtypes.float4_e2m1fn).view(np.uint8) & 0xF
        words = (c[..., 0::2] | (c[..., 1::2] << 4)).reshape(k // 512, 128, 2 * n)
    return np.ascontiguousarray(words), np.ascontiguousarray(byte.astype(np.uint8).reshape(k // 512, 16, n))


def unpack_weight(words, scales, fmt):
    g, _, n = scales.shape
    words = np.ascontiguousarray(words).reshape(g, 128, n, -1)
    if fmt == "e4m3":
        vals = words.view(ml_dtypes.float8_e4m3fn).astype(np.float64)
    else:
        nib = np.empty((g, 128, n, 4), np.uint8)
        nib[..., 0::2] = words & 0xF
        nib[..., 1::2] = words >> 4
        vals = E2M1[nib]
    vals = vals * np.repeat(np.exp2(scales.astype(np.float64) - 127.0), 8, axis=1)[..., None]
    return vals.transpose(0, 1, 3, 2).reshape(g * 512, n)


def relu(v):
    return np.maximum(v, 0.0)


K, T, E, C = 512, 768, 6, 256


def deal():
    first = np.random.permutation(np.repeat(np.arange(E), T // E))
    second = (first + 1 + np.random.permutation(np.repeat(np.arange(E - 1), -(-T // (E - 1)))[:T])) % E
    while np.bincount(second, minlength=E).max() != T // E:
        load = np.bincount(second, minlength=E); hi, lo = int(load.argmax()), int(load.argmin())
        t = np.flatnonzero((second == hi) & (first != lo))[0]; second[t] = lo
    slot_token = np.empty(E * C, np.int64); pos = np.empty((2, T), np.int64); fill = np.zeros(E, np.int64)
    place = np.stack([np.random.permutation(C) for _ in range(E)])
    for r, deal in enumerate((first, second)):
        for t in np.random.permutation(T):
            e = deal[t]; j = e * C + place[e, fill[e]]; fill[e] += 1; slot_token[j] = t; pos[r, t] = j
    g = np.random.uniform(0.2, 0.8, T)
    return slot_token, pos, np.stack([g, 1.0 - g])


def by_expert(wq, xq):
    return np.concatenate([wq[e].T @ xq[:, e * C:(e + 1) * C] for e in range(E)], axis=1)


def setup_inputs():
    n = np.random.standard_normal
    s = mx_kscale(K)
    slots1, pos1, g1 = deal()
    slots2, pos2, g2 = deal()
    x = pack_weight(n((K, T)) * s[:, None], "e4m3")
    w = [pack_weight(m, "e4m3") for m in n((E, K, K)) / np.sqrt(K) / s[None, :, None] * s]
    return {
        "x_words": x[0],
        "x_scales": x[1],
        "w_words": np.stack([m[0] for m in w]),
        "w_scales": np.stack([m[1] for m in w]),
        "gate1": (np.stack([np.tile(r, (128, 1)) for r in g1])).astype(np.float32),
        "gate2": (np.stack([np.tile(r, (128, 1)) for r in g2])).astype(np.float32),
        "offs": striped(slots1),
        "pos1": striped(pos1[0]),
        "pos2": striped(pos1[1]),
        "offs2": striped(slots2),
        "pos3": striped(pos2[0]),
        "pos4": striped(pos2[1]),
    }


def reference(x_words, x_scales, w_words, w_scales, gate1, gate2, offs, pos1, pos2, offs2, pos3, pos4):
    w = np.stack([unpack_weight(w_words[e], w_scales[e], "e4m3") for e in range(E)])
    idx, idx2 = unstriped(offs), unstriped(offs2)
    y = relu(by_expert(w, unpack_weight(x_words, x_scales, "e4m3")[:, idx]))
    c = sum(f64(gate1[r, :1]) * y[:, unstriped(p)] for r, p in enumerate((pos1, pos2)))
    z = relu(by_expert(w, mxq(c[:, idx2], 0, "e4m3")))
    out = sum(f64(gate2[r, :1]) * z[:, unstriped(p)] for r, p in enumerate((pos3, pos4)))
    return out

@@ -1,0 +1,214 @@
+from contextlib import ExitStack
+
+import concourse.mybir as mybir
+
+K, T, E, C = 512, 768, 6, 256
+S = E * C
+P = 128
+PACK = 4
+FLOPS = 2 * 2 * K * K * S
+
+F32 = mybir.dt.float32
+BF16 = mybir.dt.bfloat16
+I32 = mybir.dt.int32
+U32 = mybir.dt.uint32
+U16 = mybir.dt.uint16
+U8 = mybir.dt.uint8
+FP8X4 = mybir.dt.float8_e4m3fn_x4
+MULT = mybir.AluOpType.mult
+ADD = mybir.AluOpType.add
+RELU = mybir.ActivationFunctionType.Relu
+COPY = mybir.ActivationFunctionType.Copy
+
+
+def tile_moe_uni_relu_kernel(
+    tc, x_words, x_scales, w_words, w_scales, gate1, gate2, offs, pos1, pos2, offs2, pos3, pos4, out
+):
+    nc = tc.nc
+    with ExitStack() as ctx:
+        keep = ctx.enter_context(tc.tile_pool(name="keep", bufs=1))
+        ring = ctx.enter_context(tc.tile_pool(name="ring", bufs=2))
+        psum = ctx.enter_context(tc.psum_pool(name="psum", bufs=4))
+
+        def load_list(src, name):
+            tile = keep.tile(list(src.shape), U16, name=name)
+            nc.sync.dma_start(tile[:], src)
+            return tile
+
+        def entries(tile, lo, hi):
+            return tile[:, lo // 16 : hi // 16]
+
+        xs = keep.tile([P, T], U8, name="xs", align_bytes=64)
+        ws_raw = keep.tile([P, 2 * K], U8, name="ws_raw", align_bytes=64)
+        nc.vector.memset(xs[:].bitcast(I32), 0)
+        nc.vector.memset(ws_raw[:].bitcast(I32), 0)
+
+        offs_t = load_list(offs, "offs_t")
+        xw = keep.tile([P, T], I32, name="xw", align_bytes=64)
+        nc.scalar.dma_start(xw[:], x_words[0].rearrange("p t d -> p (t d)").bitcast(I32))
+        for q in range(4):
+            nc.sync.dma_start(xs[32 * q : 32 * q + 4, :].bitcast(I32), x_scales[0, 4 * q : 4 * q + 4, :].bitcast(I32))
+
+        w_raw = [keep.tile([P, 2, K], I32, name=f"w_raw{a}", align_bytes=64) for a in range(3)]
+
+        def load_w(a):
+            nc.sync.dma_start(
+                w_raw[a][:], w_words[2 * a : 2 * a + 2, 0].rearrange("e p i d -> p e (i d)").bitcast(I32)
+            )
+
+        def load_ws(g):
+            n = (4, 2)[g]
+            for q in range(4):
+                nc.sync.dma_start(
+                    ws_raw[32 * q : 32 * q + 4 * n, g * K : (g + 1) * K].bitcast(I32),
+                    w_scales[4 * g : 4 * g + n, 0, 4 * q : 4 * q + 4, :].bitcast(I32),
+                )
+
+        load_w(0)
+        load_ws(0)
+        load_ws(1)
+        load_w(1)
+        load_w(2)
+        pos1_t = load_list(pos1, "pos1_t")
+        pos2_t = load_list(pos2, "pos2_t")
+        g1 = keep.tile([P, 2, T], F32, name="g1")
+        nc.sync.dma_start(g1[:], gate1.rearrange("r p t -> p r t"))
+        offs2_t = load_list(offs2, "offs2_t")
+        pos3_t = load_list(pos3, "pos3_t")
+        pos4_t = load_list(pos4, "pos4_t")
+        g2 = keep.tile([P, 2, T], F32, name="g2")
+        nc.sync.dma_start(g2[:], gate2.rearrange("r p t -> p r t"))
+
+        wp = [keep.tile([P, PACK, 2 * P], I32, name=f"wp{a}", align_bytes=64) for a in range(3)]
+        wsp = keep.tile([P, PACK, 2 * P], U8, name="wsp", align_bytes=64)
+
+        def permute_w(a):
+            nc.vector.tensor_copy(
+                wp[a][:].rearrange("p t (g i) -> p g t i", i=4),
+                w_raw[a][:].rearrange("p e (g i t) -> p (e g) t i", i=4, t=PACK),
+            )
+
+        def permute_ws():
+            nc.vector.tensor_copy(
+                wsp[:].rearrange("p t (g i) -> p g t i", i=16),
+                ws_raw[:].rearrange("p (g i t) -> p g t i", i=16, t=PACK),
+            )
+
+        def expert_matmul(acc, e, t, codes, scales):
+            g, k = divmod(e, 4)
+            nc.tensor.matmul_mx(
+                out=acc,
+                lhsT=wp[e // 2][:, t, (e % 2) * P : (e % 2 + 1) * P].bitcast(FP8X4),
+                lhsT_scale=wsp[4 * k : P, t, g * P : (g + 1) * P],
+                rhs=codes.bitcast(FP8X4),
+                rhs_scale=scales,
+                start=True,
+                stop=True,
+            )
+
+        def experts(res, es, t, operand, tag):
+            acc = psum.tile([P, 2 * C], F32, name=tag)
+            for n, e in enumerate(es):
+                expert_matmul(acc[:, n * C : (n + 1) * C], e, t, *operand(e))
+            nc.scalar.activation(res[t][:, es[0] * C : (es[-1] + 1) * C], acc[:, : len(es) * C], RELU)
+
+        xg_w = [keep.tile([P, 2 * C], U32, name=f"xg_w{a}", align_bytes=64) for a in range(3)]
+        xg_s = [keep.tile([P, 2 * C], U8, name=f"xg_s{a}", align_bytes=64) for a in range(3)]
+
+        def gather_x(a, lo, hi):
+            sl = entries(offs_t, 2 * C * a + lo, 2 * C * a + hi)
+            nc.vector.tensor_copy(xg_s[a][:, lo:hi], xs[:].indirect(sl))
+            nc.vector.tensor_copy(xg_w[a][:, lo:hi], xw[:].bitcast(U32).indirect(sl))
+
+        def x_operand(e):
+            cols = slice((e % 2) * C, (e % 2 + 1) * C)
+            return xg_w[e // 2][:, cols], xg_s[e // 2][:, cols]
+
+        y = [keep.tile([P, S], F32, name=f"y{t}") for t in range(PACK)]
+        gather_x(0, 0, 2 * C)
+        permute_w(0)
+        permute_ws()
+        for t in range(PACK):
+            experts(y, (0, 1), t, x_operand, "first" if t == 0 else "rest")
+        gather_x(1, 0, 2 * C)
+        permute_w(1)
+        for t in range(PACK):
+            experts(y, (2, 3), t, x_operand, "first" if t == 0 else "rest")
+        permute_w(2)
+        gather_x(2, 0, C)
+        experts(y, (4,), 0, x_operand, "first")
+        gather_x(2, C, 2 * C)
+        experts(y, (5,), 0, x_operand, "first")
+        for t in range(1, PACK):
+            experts(y, (4, 5), t, x_operand, "rest")
+
+        def gated(dst, src, lst, gate, lo, hi):
+            nc.vector.tensor_tensor(dst[:, lo:hi], src[:].indirect(entries(lst, lo, hi)), gate[:, lo:hi], MULT)
+
+        c = keep.tile([P, PACK, T], BF16, name="c", align_bytes=64)
+        cg = [keep.tile([P, 2, C, 2], BF16, name=f"cg{e}", align_bytes=64) for e in range(E)]
+
+        def gather_c(e, t):
+            nc.scalar.activation(
+                cg[e][:, t // 2, :, t % 2], c[:, t, :].indirect(entries(offs2_t, e * C, (e + 1) * C)), COPY
+            )
+
+        LEAD = 256
+        a_next = ring.tile([P, T], F32, name="first_term")
+        gated(a_next, y[0], pos1_t, g1[:, 0, :], 0, T)
+        for t in range(PACK):
+            a_cur = a_next
+            b_cur = ring.tile([P, T], F32, name="second_term")
+            if t < PACK - 1:
+                gated(b_cur, y[t], pos2_t, g1[:, 1, :], 0, T)
+                a_next = ring.tile([P, T], F32, name="first_term")
+                gated(a_next, y[t + 1], pos1_t, g1[:, 0, :], 0, LEAD)
+                nc.vector.tensor_tensor(c[:, t, :], a_cur[:], b_cur[:], ADD)
+                gated(a_next, y[t + 1], pos1_t, g1[:, 0, :], LEAD, T)
+                for e in range(E):
+                    gather_c(e, t)
+            else:
+                for lo, hi in ((0, 512), (512, T)):
+                    gated(b_cur, y[t], pos2_t, g1[:, 1, :], lo, hi)
+                for lo, hi in ((0, 512), (512, T)):
+                    nc.vector.tensor_tensor(c[:, t, lo:hi], a_cur[:, lo:hi], b_cur[:, lo:hi], ADD)
+
+        cq = [keep.tile([P, C, 2, 2], BF16, name=f"cq{e}", align_bytes=64) for e in range(E)]
+        cw = [keep.tile([P, C], U32, name=f"cw{e}", align_bytes=64) for e in range(E)]
+        cs = [keep.tile([P, C], U8, name=f"cs{e}", align_bytes=64) for e in range(E)]
+        z = [keep.tile([P, S], F32, name=f"z{t}") for t in range(PACK)]
+
+        def c_operand(e):
+            return cw[e][:], cs[e][:]
+
+        for e in range(E):
+            gather_c(e, PACK - 1)
+        for e in range(E):
+            nc.vector.tensor_copy(cq[e][:], cg[e][:].rearrange("p u s d -> p s u d"))
+            nc.vector.quantize_mx(
+                out=cw[e][:].bitcast(FP8X4), scales=cs[e][:], in_=cq[e][:].rearrange("p s u d -> p (s u d)")
+            )
+        for es in ((0, 1), (2, 3), (4,), (5,)):
+            experts(z, es, 0, c_operand, "first")
+        for t in range(1, PACK):
+            for es in ((0, 1), (2, 3), (4, 5)):
+                experts(z, es, t, c_operand, "rest")
+
+        out_rows = out.rearrange("(p t) n -> p t n", t=PACK)
+        pieces = [(t, 0, T) for t in range(PACK - 1)] + [(PACK - 1, 0, 512), (PACK - 1, 512, T)]
+        pending = None
+        for t, lo, hi in pieces:
+            a_cur = ring.tile([P, T], F32, name="first_term")
+            b_cur = ring.tile([P, T], F32, name="second_term")
+            gated(a_cur, z[t], pos3_t, g2[:, 0, :], lo, hi)
+            if pending is not None:
+                pending()
+            gated(b_cur, z[t], pos4_t, g2[:, 1, :], lo, hi)
+
+            def finish(t=t, lo=lo, hi=hi, a=a_cur, b=b_cur):
+                res = ring.tile([P, T], F32, name="res")
+                nc.vector.tensor_tensor(res[:, lo:hi], a[:, lo:hi], b[:, lo:hi], ADD)
+                nc.sync.dma_start(out_rows[:, t, lo:hi], res[:, lo:hi])
+
+            pending = finish
+        pending()

@@ -1,6 +1,7 @@
 from contextlib import ExitStack
 
 import concourse.mybir as mybir
+from concourse.masks import make_identity
 
 K, T, E, C = 512, 768, 6, 256
 S = E * C
@@ -28,7 +29,7 @@ def tile_moe_uni_relu_kernel(
     with ExitStack() as ctx:
         keep = ctx.enter_context(tc.tile_pool(name="keep", bufs=1))
         ring = ctx.enter_context(tc.tile_pool(name="ring", bufs=2))
-        psum = ctx.enter_context(tc.psum_pool(name="psum", bufs=4))
+        psum = ctx.enter_context(tc.psum_pool(name="psum", bufs=1))
 
         def load_list(src, name):
             tile = keep.tile(list(src.shape), U16, name=name)
@@ -39,17 +40,20 @@ def tile_moe_uni_relu_kernel(
             return tile[:, lo // 16 : hi // 16]
 
         xs = keep.tile([P, T], U8, name="xs", align_bytes=64)
-        ws_raw = keep.tile([P, 2 * K], U8, name="ws_raw", align_bytes=64)
-        nc.vector.memset(xs[:].bitcast(I32), 0)
-        nc.vector.memset(ws_raw[:].bitcast(I32), 0)
+        ws_raw = [keep.tile([P, K], U8, name=f"ws_raw{g}", tag=f"ws_raw{g}", align_bytes=64) for g in range(2)]
+        for g in range(2):
+            nc.vector.memset(ws_raw[g][:].bitcast(I32), 0)
 
         offs_t = load_list(offs, "offs_t")
         xw = keep.tile([P, T], I32, name="xw", align_bytes=64)
-        nc.scalar.dma_start(xw[:], x_words[0].rearrange("p t d -> p (t d)").bitcast(I32))
+        nc.sync.dma_start(xw[:], x_words[0].rearrange("p t d -> p (t d)").bitcast(I32))
         for q in range(4):
-            nc.sync.dma_start(xs[32 * q : 32 * q + 4, :].bitcast(I32), x_scales[0, 4 * q : 4 * q + 4, :].bitcast(I32))
+            nc.scalar.dma_start(
+                xs[32 * q : 32 * q + 32, :].bitcast(I32),
+                x_scales[0, 4 * q : 4 * q + 4, :].bitcast(I32).partition_broadcast(8),
+            )
 
-        w_raw = [keep.tile([P, 2, K], I32, name=f"w_raw{a}", align_bytes=64) for a in range(3)]
+        w_raw = [keep.tile([P, 2, K], I32, name=f"w_raw{a}", tag=f"w_raw{a}", align_bytes=64) for a in range(3)]
 
         def load_w(a):
             nc.sync.dma_start(
@@ -60,14 +64,14 @@ def tile_moe_uni_relu_kernel(
             n = (4, 2)[g]
             for q in range(4):
                 nc.sync.dma_start(
-                    ws_raw[32 * q : 32 * q + 4 * n, g * K : (g + 1) * K].bitcast(I32),
+                    ws_raw[g][32 * q : 32 * q + 4 * n, :].bitcast(I32),
                     w_scales[4 * g : 4 * g + n, 0, 4 * q : 4 * q + 4, :].bitcast(I32),
                 )
 
         load_w(0)
         load_ws(0)
-        load_ws(1)
         load_w(1)
+        load_ws(1)
         load_w(2)
         pos1_t = load_list(pos1, "pos1_t")
         pos2_t = load_list(pos2, "pos2_t")
@@ -80,7 +84,9 @@ def tile_moe_uni_relu_kernel(
         nc.sync.dma_start(g2[:], gate2.rearrange("r p t -> p r t"))
 
         wp = [keep.tile([P, PACK, 2 * P], I32, name=f"wp{a}", align_bytes=64) for a in range(3)]
-        wsp = keep.tile([P, PACK, 2 * P], U8, name="wsp", align_bytes=64)
+        wsp = keep.tile([P, 2, PACK, P], U8, name="wsp", align_bytes=64)
+        ident = keep.tile([P, P], F32, name="ident")
+        make_identity(nc, ident[:])
 
         def permute_w(a):
             nc.vector.tensor_copy(
@@ -88,10 +94,10 @@ def tile_moe_uni_relu_kernel(
                 w_raw[a][:].rearrange("p e (g i t) -> p (e g) t i", i=4, t=PACK),
             )
 
-        def permute_ws():
+        def permute_ws(g):
             nc.vector.tensor_copy(
-                wsp[:].rearrange("p t (g i) -> p g t i", i=16),
-                ws_raw[:].rearrange("p (g i t) -> p g t i", i=16, t=PACK),
+                wsp[:, g].rearrange("p t (g i) -> p g t i", i=16),
+                ws_raw[g][:].rearrange("p (g i t) -> p g t i", i=16, t=PACK),
             )
 
         def expert_matmul(acc, e, t, codes, scales):
@@ -99,48 +105,62 @@ def tile_moe_uni_relu_kernel(
             nc.tensor.matmul_mx(
                 out=acc,
                 lhsT=wp[e // 2][:, t, (e % 2) * P : (e % 2 + 1) * P].bitcast(FP8X4),
-                lhsT_scale=wsp[4 * k : P, t, g * P : (g + 1) * P],
+                lhsT_scale=wsp[4 * k : P, g, t, :],
                 rhs=codes.bitcast(FP8X4),
                 rhs_scale=scales,
                 start=True,
                 stop=True,
             )
 
-        def experts(res, es, t, operand, tag):
-            acc = psum.tile([P, 2 * C], F32, name=tag)
+        def bank(b):
+            return psum.tile([P, 2 * C], F32, name=f"bank{b}")
+
+        def experts(res, es, t, operand, b, on_vector=False):
+            acc = bank(b)
             for n, e in enumerate(es):
                 expert_matmul(acc[:, n * C : (n + 1) * C], e, t, *operand(e))
-            nc.scalar.activation(res[t][:, es[0] * C : (es[-1] + 1) * C], acc[:, : len(es) * C], RELU)
+            dst, src = res[t][:, es[0] * C : (es[-1] + 1) * C], acc[:, : len(es) * C]
+            if on_vector:
+                nc.vector.tensor_scalar_max(dst, src, 0.0)
+            else:
+                nc.scalar.activation(dst, src, RELU)
 
-        xg_w = [keep.tile([P, 2 * C], U32, name=f"xg_w{a}", align_bytes=64) for a in range(3)]
-        xg_s = [keep.tile([P, 2 * C], U8, name=f"xg_s{a}", align_bytes=64) for a in range(3)]
+        def gather_x(into, window, dtype, es, tag):
+            dst = keep.tile([P, len(es) * C], dtype, name=f"gathered_{tag}", tag=tag, align_bytes=64)
+            nc.vector.tensor_copy(dst[:], window.indirect(entries(offs_t, es[0] * C, (es[-1] + 1) * C)))
+            for n, e in enumerate(es):
+                into[e] = dst[:, n * C : (n + 1) * C]
 
-        def gather_x(a, lo, hi):
-            sl = entries(offs_t, 2 * C * a + lo, 2 * C * a + hi)
-            nc.vector.tensor_copy(xg_s[a][:, lo:hi], xs[:].indirect(sl))
-            nc.vector.tensor_copy(xg_w[a][:, lo:hi], xw[:].bitcast(U32).indirect(sl))
+        xg_w, xg_s = {}, {}
+
+        def gather_words(es, tag):
+            gather_x(xg_w, xw[:].bitcast(U32), U32, es, tag)
+
+        def gather_scales(es, tag):
+            gather_x(xg_s, xs[:], U8, es, tag)
 
         def x_operand(e):
-            cols = slice((e % 2) * C, (e % 2 + 1) * C)
-            return xg_w[e // 2][:, cols], xg_s[e // 2][:, cols]
+            return xg_w[e], xg_s[e]
 
         y = [keep.tile([P, S], F32, name=f"y{t}") for t in range(PACK)]
-        gather_x(0, 0, 2 * C)
+        gather_scales((0, 1), "xg_s")
+        gather_words((0, 1), "xg_w")
         permute_w(0)
-        permute_ws()
-        for t in range(PACK):
-            experts(y, (0, 1), t, x_operand, "first" if t == 0 else "rest")
-        gather_x(1, 0, 2 * C)
+        permute_ws(0)
+        experts(y, (0, 1), 0, x_operand, 0)
+        gather_words((2, 3), "w_raw0")
+        gather_scales((2, 3), "ws_raw0")
         permute_w(1)
-        for t in range(PACK):
-            experts(y, (2, 3), t, x_operand, "first" if t == 0 else "rest")
+        experts(y, (2, 3), 0, x_operand, 1)
+        gather_words((4,), "w_raw1")
         permute_w(2)
-        gather_x(2, 0, C)
-        experts(y, (4,), 0, x_operand, "first")
-        gather_x(2, C, 2 * C)
-        experts(y, (5,), 0, x_operand, "first")
-        for t in range(1, PACK):
-            experts(y, (4, 5), t, x_operand, "rest")
+        permute_ws(1)
+        gather_scales((4, 5), "ws_raw1")
+        experts(y, (4,), 0, x_operand, 2)
+        gather_words((5,), "w_raw2")
+        experts(y, (5,), 0, x_operand, 3)
+        for n, (es, t) in enumerate((es, t) for es in ((0, 1), (2, 3), (4, 5)) for t in range(1, PACK)):
+            experts(y, es, t, x_operand, 4 + n % 4)
 
         def gated(dst, src, lst, gate, lo, hi):
             nc.vector.tensor_tensor(dst[:, lo:hi], src[:].indirect(entries(lst, lo, hi)), gate[:, lo:hi], MULT)
@@ -188,27 +208,58 @@ def tile_moe_uni_relu_kernel(
             nc.vector.quantize_mx(
                 out=cw[e][:].bitcast(FP8X4), scales=cs[e][:], in_=cq[e][:].rearrange("p s u d -> p (s u d)")
             )
-        for es in ((0, 1), (2, 3), (4,), (5,)):
-            experts(z, es, 0, c_operand, "first")
-        for t in range(1, PACK):
-            for es in ((0, 1), (2, 3), (4, 5)):
-                experts(z, es, t, c_operand, "rest")
+        for b, es in enumerate(((0, 1), (2, 3), (4,), (5,))):
+            experts(z, es, 0, c_operand, b, on_vector=len(es) == 1)
+        for n, (es, t) in enumerate((es, t) for t in range(1, PACK) for es in ((0, 1), (2, 3), (4, 5))):
+            experts(z, es, t, c_operand, 4 + n % 4)
 
         out_rows = out.rearrange("(p t) n -> p t n", t=PACK)
-        pieces = [(t, 0, T) for t in range(PACK - 1)] + [(PACK - 1, 0, 512), (PACK - 1, 512, T)]
-        pending = None
-        for t, lo, hi in pieces:
+        HALVES = ((0, 512), (512, T))
+
+        def turn(acc, src, lo, hi, start, stop):
+            for s0 in range(lo, hi, P):
+                nc.tensor.matmul(
+                    acc[:, s0 - lo : s0 - lo + P],
+                    lhsT=src[:, s0 : s0 + P],
+                    rhs=ident[:],
+                    is_transpose=True,
+                    start=start and s0 == lo,
+                    stop=stop and s0 == hi - P,
+                )
+
+        for t in range(PACK - 1):
             a_cur = ring.tile([P, T], F32, name="first_term")
             b_cur = ring.tile([P, T], F32, name="second_term")
-            gated(a_cur, z[t], pos3_t, g2[:, 0, :], lo, hi)
-            if pending is not None:
-                pending()
-            gated(b_cur, z[t], pos4_t, g2[:, 1, :], lo, hi)
+            gated(a_cur, z[t], pos3_t, g2[:, 0, :], 0, T)
+            gated(b_cur, z[t], pos4_t, g2[:, 1, :], 0, T)
+            sums = [bank(0), bank(1)]
+            for acc, (lo, hi) in zip(sums, HALVES):
+                turn(acc, a_cur, lo, hi, True, False)
+            for acc, (lo, hi) in zip(sums, HALVES):
+                turn(acc, b_cur, lo, hi, False, True)
+            sum_t = ring.tile([P, T], F32, name="sum_t")
+            res = ring.tile([P, T], F32, name="res")
+            for acc, (lo, hi) in zip(sums, HALVES):
+                nc.scalar.activation(sum_t[:, lo:hi], acc[:, : hi - lo], COPY)
+            for h, (lo, hi) in enumerate(HALVES):
+                back = bank(2 + h)
+                for s0 in range(lo, hi, P):
+                    nc.tensor.transpose(back[:, s0 - lo : s0 - lo + P], sum_t[:, s0 : s0 + P], ident[:])
+                nc.scalar.activation(res[:, lo:hi], back[:, : hi - lo], COPY)
+                nc.scalar.dma_start(out_rows[:, t, lo:hi], res[:, lo:hi])
 
-            def finish(t=t, lo=lo, hi=hi, a=a_cur, b=b_cur):
-                res = ring.tile([P, T], F32, name="res")
-                nc.vector.tensor_tensor(res[:, lo:hi], a[:, lo:hi], b[:, lo:hi], ADD)
-                nc.sync.dma_start(out_rows[:, t, lo:hi], res[:, lo:hi])
+        t = PACK - 1
+        a_cur = ring.tile([P, T], F32, name="first_term")
+        b_cur = ring.tile([P, T], F32, name="second_term")
+        last = ring.tile([P, T], F32, name="last")
 
-            pending = finish
-        pending()
+        def finish(lo, hi):
+            nc.vector.tensor_tensor(last[:, lo:hi], a_cur[:, lo:hi], b_cur[:, lo:hi], ADD)
+            nc.sync.dma_start(out_rows[:, t, lo:hi], last[:, lo:hi])
+
+        gated(a_cur, z[t], pos3_t, g2[:, 0, :], *HALVES[0])
+        gated(b_cur, z[t], pos4_t, g2[:, 1, :], *HALVES[0])
+        gated(a_cur, z[t], pos3_t, g2[:, 0, :], *HALVES[1])
+        finish(*HALVES[0])
+        gated(b_cur, z[t], pos4_t, g2[:, 1, :], *HALVES[1])
+        finish(*HALVES[1])

@@ -45,10 +45,8 @@ def tile_moe_uni_relu_kernel(
             nc.vector.memset(ws_raw[g][:].bitcast(I32), 0)
 
         offs_t = load_list(offs, "offs_t")
-        xw = keep.tile([P, T], I32, name="xw", align_bytes=64)
-        nc.sync.dma_start(xw[:], x_words[0].rearrange("p t d -> p (t d)").bitcast(I32))
         for q in range(4):
-            nc.scalar.dma_start(
+            (nc.sync, nc.scalar)[q // 2].dma_start(
                 xs[32 * q : 32 * q + 32, :].bitcast(I32),
                 x_scales[0, 4 * q : 4 * q + 4, :].bitcast(I32).partition_broadcast(8),
             )
@@ -71,8 +69,10 @@ def tile_moe_uni_relu_kernel(
         load_w(0)
         load_ws(0)
         load_w(1)
-        load_ws(1)
         load_w(2)
+        load_ws(1)
+        xw = keep.tile([P, T], I32, name="xw", tag="xw", align_bytes=64)
+        nc.sync.dma_start(xw[:], x_words[0].rearrange("p t d -> p (t d)").bitcast(I32))
         pos1_t = load_list(pos1, "pos1_t")
         pos2_t = load_list(pos2, "pos2_t")
         g1 = keep.tile([P, 2, T], F32, name="g1")
@@ -83,29 +83,31 @@ def tile_moe_uni_relu_kernel(
         g2 = keep.tile([P, 2, T], F32, name="g2")
         nc.sync.dma_start(g2[:], gate2.rearrange("r p t -> p r t"))
 
-        wp = [keep.tile([P, PACK, 2 * P], I32, name=f"wp{a}", align_bytes=64) for a in range(3)]
-        wsp = keep.tile([P, 2, PACK, P], U8, name="wsp", align_bytes=64)
+        wp = {}
+        wsp = {}
         ident = keep.tile([P, P], F32, name="ident")
         make_identity(nc, ident[:])
 
-        def permute_w(a):
+        def permute_w(dst, a, u):
             nc.vector.tensor_copy(
-                wp[a][:].rearrange("p t (g i) -> p g t i", i=4),
-                w_raw[a][:].rearrange("p e (g i t) -> p (e g) t i", i=4, t=PACK),
+                dst.rearrange("p t (g i) -> p g t i", i=4),
+                w_raw[a][:].rearrange("p e (g i t) -> p (e g) t i", i=4, t=PACK)[:, :, 2 * u : 2 * u + 2, :],
             )
+            wp[a, u] = dst
 
-        def permute_ws(g):
+        def permute_ws(dst, g, u):
             nc.vector.tensor_copy(
-                wsp[:, g].rearrange("p t (g i) -> p g t i", i=16),
-                ws_raw[g][:].rearrange("p (g i t) -> p g t i", i=16, t=PACK),
+                dst.rearrange("p t (g i) -> p g t i", i=16),
+                ws_raw[g][:].rearrange("p (g i t) -> p g t i", i=16, t=PACK)[:, :, 2 * u : 2 * u + 2, :],
             )
+            wsp[g, u] = dst
 
         def expert_matmul(acc, e, t, codes, scales):
             g, k = divmod(e, 4)
             nc.tensor.matmul_mx(
                 out=acc,
-                lhsT=wp[e // 2][:, t, (e % 2) * P : (e % 2 + 1) * P].bitcast(FP8X4),
-                lhsT_scale=wsp[4 * k : P, g, t, :],
+                lhsT=wp[e // 2, t // 2][:, t % 2, (e % 2) * P : (e % 2 + 1) * P].bitcast(FP8X4),
+                lhsT_scale=wsp[g, t // 2][4 * k : P, t % 2, :],
                 rhs=codes.bitcast(FP8X4),
                 rhs_scale=scales,
                 start=True,
@@ -125,52 +127,52 @@ def tile_moe_uni_relu_kernel(
             else:
                 nc.scalar.activation(dst, src, RELU)
 
-        def gather_x(into, window, dtype, es, tag):
-            dst = keep.tile([P, len(es) * C], dtype, name=f"gathered_{tag}", tag=tag, align_bytes=64)
-            nc.vector.tensor_copy(dst[:], window.indirect(entries(offs_t, es[0] * C, (es[-1] + 1) * C)))
-            for n, e in enumerate(es):
-                into[e] = dst[:, n * C : (n + 1) * C]
-
         xg_w, xg_s = {}, {}
 
-        def gather_words(es, tag):
-            gather_x(xg_w, xw[:].bitcast(U32), U32, es, tag)
-
-        def gather_scales(es, tag):
-            gather_x(xg_s, xs[:], U8, es, tag)
+        def gather_x(into, window, dst, es):
+            nc.vector.tensor_copy(dst, window.indirect(entries(offs_t, es[0] * C, (es[-1] + 1) * C)))
+            for n, e in enumerate(es):
+                into[e] = dst[:, n * C : (n + 1) * C]
 
         def x_operand(e):
             return xg_w[e], xg_s[e]
 
         y = [keep.tile([P, S], F32, name=f"y{t}") for t in range(PACK)]
-        gather_scales((0, 1), "xg_s")
-        gather_words((0, 1), "xg_w")
-        permute_w(0)
-        permute_ws(0)
-        experts(y, (0, 1), 0, x_operand, 0)
-        gather_words((2, 3), "w_raw0")
-        gather_scales((2, 3), "ws_raw0")
-        permute_w(1)
-        experts(y, (2, 3), 0, x_operand, 1)
-        gather_words((4,), "w_raw1")
-        permute_w(2)
-        permute_ws(1)
-        gather_scales((4, 5), "ws_raw1")
-        experts(y, (4,), 0, x_operand, 2)
-        gather_words((5,), "w_raw2")
-        experts(y, (5,), 0, x_operand, 3)
-        for n, (es, t) in enumerate((es, t) for es in ((0, 1), (2, 3), (4, 5)) for t in range(1, PACK)):
+        words = xw[:].bitcast(U32)
+        early = keep.tile([P, 3, 2, 2 * P], I32, name="early", align_bytes=64)
+        scales_g = keep.tile([P, S], U8, name="scales_g", align_bytes=64)
+        for a in range(3):
+            gather_x(xg_s, xs[:], scales_g[:, 2 * C * a : 2 * C * (a + 1)], (2 * a, 2 * a + 1))
+        early_s = keep.tile([P, 2, 2, P], U8, name="early_s", align_bytes=64)
+        for a in range(3):
+            permute_w(early[:, a], a, 0)
+        for g in range(2):
+            permute_ws(early_s[:, g], g, 0)
+        words_g = keep.tile([P, S], U32, name="words_g", align_bytes=64)
+        for b, es in enumerate(((0, 1), (2, 3), (4,), (5,))):
+            gather_x(xg_w, words, words_g[:, es[0] * C : (es[-1] + 1) * C], es)
+            experts(y, es, 0, x_operand, b)
+        late_all = keep.tile([P, 3 * K + P], I32, name="late_all", tag="xw", align_bytes=64)
+        late = late_all[:, : 3 * K].rearrange("p (a t m) -> p a t m", a=3, t=2)
+        late_s = late_all[:, 3 * K :].bitcast(U8).rearrange("p (g t m) -> p g t m", g=2, t=2)
+        for a in range(3):
+            permute_w(late[:, a], a, 1)
+        for g in range(2):
+            permute_ws(late_s[:, g], g, 1)
+        for n, (es, t) in enumerate((es, t) for t in range(1, PACK) for es in ((0, 1), (2, 3), (4, 5))):
             experts(y, es, t, x_operand, 4 + n % 4)
 
         def gated(dst, src, lst, gate, lo, hi):
             nc.vector.tensor_tensor(dst[:, lo:hi], src[:].indirect(entries(lst, lo, hi)), gate[:, lo:hi], MULT)
 
         c = keep.tile([P, PACK, T], BF16, name="c", align_bytes=64)
-        cg = [keep.tile([P, 2, C, 2], BF16, name=f"cg{e}", align_bytes=64) for e in range(E)]
+        cg = [keep.tile([P, 2, C, 2], BF16, name=f"cg{e}", align_bytes=64) for e in range(E - 1)]
+        cq = [keep.tile([P, C, 2, 2], BF16, name=f"cq{e}", align_bytes=64) for e in range(E)]
 
         def gather_c(e, t):
+            dst = cg[e][:, t // 2, :, t % 2] if e < E - 1 else cq[e][:, :, t // 2, t % 2]
             nc.scalar.activation(
-                cg[e][:, t // 2, :, t % 2], c[:, t, :].indirect(entries(offs2_t, e * C, (e + 1) * C)), COPY
+                dst, c[:, t, :].indirect(entries(offs2_t, e * C, (e + 1) * C)), COPY
             )
 
         LEAD = 256
@@ -193,7 +195,6 @@ def tile_moe_uni_relu_kernel(
                 for lo, hi in ((0, 512), (512, T)):
                     nc.vector.tensor_tensor(c[:, t, lo:hi], a_cur[:, lo:hi], b_cur[:, lo:hi], ADD)
 
-        cq = [keep.tile([P, C, 2, 2], BF16, name=f"cq{e}", align_bytes=64) for e in range(E)]
         cw = [keep.tile([P, C], U32, name=f"cw{e}", align_bytes=64) for e in range(E)]
         cs = [keep.tile([P, C], U8, name=f"cs{e}", align_bytes=64) for e in range(E)]
         z = [keep.tile([P, S], F32, name=f"z{t}") for t in range(PACK)]
@@ -203,11 +204,14 @@ def tile_moe_uni_relu_kernel(
 
         for e in range(E):
             gather_c(e, PACK - 1)
-        for e in range(E):
-            nc.vector.tensor_copy(cq[e][:], cg[e][:].rearrange("p u s d -> p s u d"))
-            nc.vector.quantize_mx(
-                out=cw[e][:].bitcast(FP8X4), scales=cs[e][:], in_=cq[e][:].rearrange("p s u d -> p (s u d)")
-            )
+        for step in range(E + 1):
+            if step < E - 1:
+                nc.vector.tensor_copy(cq[step][:], cg[step][:].rearrange("p u s d -> p s u d"))
+            if step > 0:
+                e = step - 1
+                nc.vector.quantize_mx(
+                    out=cw[e][:].bitcast(FP8X4), scales=cs[e][:], in_=cq[e][:].rearrange("p s u d -> p (s u d)")
+                )
         for b, es in enumerate(((0, 1), (2, 3), (4,), (5,))):
             experts(z, es, 0, c_operand, b, on_vector=len(es) == 1)
         for n, (es, t) in enumerate((es, t) for t in range(1, PACK) for es in ((0, 1), (2, 3), (4, 5))):

from contextlib import ExitStack

import concourse.mybir as mybir
from concourse.masks import make_identity

K, T, E, C = 512, 768, 6, 256
S = E * C
P = 128
PACK = 4
FLOPS = 2 * 2 * K * K * S

F32 = mybir.dt.float32
BF16 = mybir.dt.bfloat16
I32 = mybir.dt.int32
U32 = mybir.dt.uint32
U16 = mybir.dt.uint16
U8 = mybir.dt.uint8
FP8X4 = mybir.dt.float8_e4m3fn_x4
MULT = mybir.AluOpType.mult
ADD = mybir.AluOpType.add
RELU = mybir.ActivationFunctionType.Relu
COPY = mybir.ActivationFunctionType.Copy


def tile_moe_uni_relu_kernel(
    tc, x_words, x_scales, w_words, w_scales, gate1, gate2, offs, pos1, pos2, offs2, pos3, pos4, out
):
    nc = tc.nc
    with ExitStack() as ctx:
        keep = ctx.enter_context(tc.tile_pool(name="keep", bufs=1))
        ring = ctx.enter_context(tc.tile_pool(name="ring", bufs=2))
        psum = ctx.enter_context(tc.psum_pool(name="psum", bufs=1))

        def load_list(src, name):
            tile = keep.tile(list(src.shape), U16, name=name)
            nc.sync.dma_start(tile[:], src)
            return tile

        def entries(tile, lo, hi):
            return tile[:, lo // 16 : hi // 16]

        xs = keep.tile([P, T], U8, name="xs", align_bytes=64)
        ws_raw = [keep.tile([P, K], U8, name=f"ws_raw{g}", tag=f"ws_raw{g}", align_bytes=64) for g in range(2)]
        for g in range(2):
            nc.vector.memset(ws_raw[g][:].bitcast(I32), 0)

        offs_t = load_list(offs, "offs_t")
        for q in range(4):
            (nc.sync, nc.scalar)[q // 2].dma_start(
                xs[32 * q : 32 * q + 32, :].bitcast(I32),
                x_scales[0, 4 * q : 4 * q + 4, :].bitcast(I32).partition_broadcast(8),
            )

        w_raw = [keep.tile([P, 2, K], I32, name=f"w_raw{a}", tag=f"w_raw{a}", align_bytes=64) for a in range(3)]

        def load_w(a):
            nc.sync.dma_start(
                w_raw[a][:], w_words[2 * a : 2 * a + 2, 0].rearrange("e p i d -> p e (i d)").bitcast(I32)
            )

        def load_ws(g):
            n = (4, 2)[g]
            for q in range(4):
                nc.sync.dma_start(
                    ws_raw[g][32 * q : 32 * q + 4 * n, :].bitcast(I32),
                    w_scales[4 * g : 4 * g + n, 0, 4 * q : 4 * q + 4, :].bitcast(I32),
                )

        load_w(0)
        load_ws(0)
        load_w(1)
        load_w(2)
        load_ws(1)
        xw = keep.tile([P, T], I32, name="xw", tag="xw", align_bytes=64)
        nc.sync.dma_start(xw[:], x_words[0].rearrange("p t d -> p (t d)").bitcast(I32))
        pos1_t = load_list(pos1, "pos1_t")
        pos2_t = load_list(pos2, "pos2_t")
        g1 = keep.tile([P, 2, T], F32, name="g1")
        nc.sync.dma_start(g1[:], gate1.rearrange("r p t -> p r t"))
        offs2_t = load_list(offs2, "offs2_t")
        pos3_t = load_list(pos3, "pos3_t")
        pos4_t = load_list(pos4, "pos4_t")
        g2 = keep.tile([P, 2, T], F32, name="g2")
        nc.sync.dma_start(g2[:], gate2.rearrange("r p t -> p r t"))

        wp = {}
        wsp = {}
        ident = keep.tile([P, P], F32, name="ident")
        make_identity(nc, ident[:])

        def permute_w(dst, a, u):
            nc.vector.tensor_copy(
                dst.rearrange("p t (g i) -> p g t i", i=4),
                w_raw[a][:].rearrange("p e (g i t) -> p (e g) t i", i=4, t=PACK)[:, :, 2 * u : 2 * u + 2, :],
            )
            wp[a, u] = dst

        def permute_ws(dst, g, u):
            nc.vector.tensor_copy(
                dst.rearrange("p t (g i) -> p g t i", i=16),
                ws_raw[g][:].rearrange("p (g i t) -> p g t i", i=16, t=PACK)[:, :, 2 * u : 2 * u + 2, :],
            )
            wsp[g, u] = dst

        def expert_matmul(acc, e, t, codes, scales):
            g, k = divmod(e, 4)
            nc.tensor.matmul_mx(
                out=acc,
                lhsT=wp[e // 2, t // 2][:, t % 2, (e % 2) * P : (e % 2 + 1) * P].bitcast(FP8X4),
                lhsT_scale=wsp[g, t // 2][4 * k : P, t % 2, :],
                rhs=codes.bitcast(FP8X4),
                rhs_scale=scales,
                start=True,
                stop=True,
            )

        def bank(b):
            return psum.tile([P, 2 * C], F32, name=f"bank{b}")

        def experts(res, es, t, operand, b, on_vector=False):
            acc = bank(b)
            for n, e in enumerate(es):
                expert_matmul(acc[:, n * C : (n + 1) * C], e, t, *operand(e))
            dst, src = res[t][:, es[0] * C : (es[-1] + 1) * C], acc[:, : len(es) * C]
            if on_vector:
                nc.vector.tensor_scalar_max(dst, src, 0.0)
            else:
                nc.scalar.activation(dst, src, RELU)

        xg_w, xg_s = {}, {}

        def gather_x(into, window, dst, es):
            nc.vector.tensor_copy(dst, window.indirect(entries(offs_t, es[0] * C, (es[-1] + 1) * C)))
            for n, e in enumerate(es):
                into[e] = dst[:, n * C : (n + 1) * C]

        def x_operand(e):
            return xg_w[e], xg_s[e]

        y = [keep.tile([P, S], F32, name=f"y{t}") for t in range(PACK)]
        words = xw[:].bitcast(U32)
        early = keep.tile([P, 3, 2, 2 * P], I32, name="early", align_bytes=64)
        scales_g = keep.tile([P, S], U8, name="scales_g", align_bytes=64)
        for a in range(3):
            gather_x(xg_s, xs[:], scales_g[:, 2 * C * a : 2 * C * (a + 1)], (2 * a, 2 * a + 1))
        early_s = keep.tile([P, 2, 2, P], U8, name="early_s", align_bytes=64)
        for a in range(3):
            permute_w(early[:, a], a, 0)
        for g in range(2):
            permute_ws(early_s[:, g], g, 0)
        words_g = keep.tile([P, S], U32, name="words_g", align_bytes=64)
        for b, es in enumerate(((0, 1), (2, 3), (4,), (5,))):
            gather_x(xg_w, words, words_g[:, es[0] * C : (es[-1] + 1) * C], es)
            experts(y, es, 0, x_operand, b)
        late_all = keep.tile([P, 3 * K + P], I32, name="late_all", tag="xw", align_bytes=64)
        late = late_all[:, : 3 * K].rearrange("p (a t m) -> p a t m", a=3, t=2)
        late_s = late_all[:, 3 * K :].bitcast(U8).rearrange("p (g t m) -> p g t m", g=2, t=2)
        for a in range(3):
            permute_w(late[:, a], a, 1)
        for g in range(2):
            permute_ws(late_s[:, g], g, 1)
        for n, (es, t) in enumerate((es, t) for t in range(1, PACK) for es in ((0, 1), (2, 3), (4, 5))):
            experts(y, es, t, x_operand, 4 + n % 4)

        def gated(dst, src, lst, gate, lo, hi):
            nc.vector.tensor_tensor(dst[:, lo:hi], src[:].indirect(entries(lst, lo, hi)), gate[:, lo:hi], MULT)

        c = keep.tile([P, PACK, T], BF16, name="c", align_bytes=64)
        cg = [keep.tile([P, 2, C, 2], BF16, name=f"cg{e}", align_bytes=64) for e in range(E - 1)]
        cq = [keep.tile([P, C, 2, 2], BF16, name=f"cq{e}", align_bytes=64) for e in range(E)]

        def gather_c(e, t):
            dst = cg[e][:, t // 2, :, t % 2] if e < E - 1 else cq[e][:, :, t // 2, t % 2]
            nc.scalar.activation(
                dst, c[:, t, :].indirect(entries(offs2_t, e * C, (e + 1) * C)), COPY
            )

        LEAD = 256
        a_next = ring.tile([P, T], F32, name="first_term")
        gated(a_next, y[0], pos1_t, g1[:, 0, :], 0, T)
        for t in range(PACK):
            a_cur = a_next
            b_cur = ring.tile([P, T], F32, name="second_term")
            if t < PACK - 1:
                gated(b_cur, y[t], pos2_t, g1[:, 1, :], 0, T)
                a_next = ring.tile([P, T], F32, name="first_term")
                gated(a_next, y[t + 1], pos1_t, g1[:, 0, :], 0, LEAD)
                nc.vector.tensor_tensor(c[:, t, :], a_cur[:], b_cur[:], ADD)
                gated(a_next, y[t + 1], pos1_t, g1[:, 0, :], LEAD, T)
                for e in range(E):
                    gather_c(e, t)
            else:
                for lo, hi in ((0, 512), (512, T)):
                    gated(b_cur, y[t], pos2_t, g1[:, 1, :], lo, hi)
                for lo, hi in ((0, 512), (512, T)):
                    nc.vector.tensor_tensor(c[:, t, lo:hi], a_cur[:, lo:hi], b_cur[:, lo:hi], ADD)

        cw = [keep.tile([P, C], U32, name=f"cw{e}", align_bytes=64) for e in range(E)]
        cs = [keep.tile([P, C], U8, name=f"cs{e}", align_bytes=64) for e in range(E)]
        z = [keep.tile([P, S], F32, name=f"z{t}") for t in range(PACK)]

        def c_operand(e):
            return cw[e][:], cs[e][:]

        for e in range(E):
            gather_c(e, PACK - 1)
        for step in range(E + 1):
            if step < E - 1:
                nc.vector.tensor_copy(cq[step][:], cg[step][:].rearrange("p u s d -> p s u d"))
            if step > 0:
                e = step - 1
                nc.vector.quantize_mx(
                    out=cw[e][:].bitcast(FP8X4), scales=cs[e][:], in_=cq[e][:].rearrange("p s u d -> p (s u d)")
                )
        for b, es in enumerate(((0, 1), (2, 3), (4,), (5,))):
            experts(z, es, 0, c_operand, b, on_vector=len(es) == 1)
        for n, (es, t) in enumerate((es, t) for t in range(1, PACK) for es in ((0, 1), (2, 3), (4, 5))):
            experts(z, es, t, c_operand, 4 + n % 4)

        out_rows = out.rearrange("(p t) n -> p t n", t=PACK)
        HALVES = ((0, 512), (512, T))

        def turn(acc, src, lo, hi, start, stop):
            for s0 in range(lo, hi, P):
                nc.tensor.matmul(
                    acc[:, s0 - lo : s0 - lo + P],
                    lhsT=src[:, s0 : s0 + P],
                    rhs=ident[:],
                    is_transpose=True,
                    start=start and s0 == lo,
                    stop=stop and s0 == hi - P,
                )

        for t in range(PACK - 1):
            a_cur = ring.tile([P, T], F32, name="first_term")
            b_cur = ring.tile([P, T], F32, name="second_term")
            gated(a_cur, z[t], pos3_t, g2[:, 0, :], 0, T)
            gated(b_cur, z[t], pos4_t, g2[:, 1, :], 0, T)
            sums = [bank(0), bank(1)]
            for acc, (lo, hi) in zip(sums, HALVES):
                turn(acc, a_cur, lo, hi, True, False)
            for acc, (lo, hi) in zip(sums, HALVES):
                turn(acc, b_cur, lo, hi, False, True)
            sum_t = ring.tile([P, T], F32, name="sum_t")
            res = ring.tile([P, T], F32, name="res")
            for acc, (lo, hi) in zip(sums, HALVES):
                nc.scalar.activation(sum_t[:, lo:hi], acc[:, : hi - lo], COPY)
            for h, (lo, hi) in enumerate(HALVES):
                back = bank(2 + h)
                for s0 in range(lo, hi, P):
                    nc.tensor.transpose(back[:, s0 - lo : s0 - lo + P], sum_t[:, s0 : s0 + P], ident[:])
                nc.scalar.activation(res[:, lo:hi], back[:, : hi - lo], COPY)
                nc.scalar.dma_start(out_rows[:, t, lo:hi], res[:, lo:hi])

        t = PACK - 1
        a_cur = ring.tile([P, T], F32, name="first_term")
        b_cur = ring.tile([P, T], F32, name="second_term")
        last = ring.tile([P, T], F32, name="last")

        def finish(lo, hi):
            nc.vector.tensor_tensor(last[:, lo:hi], a_cur[:, lo:hi], b_cur[:, lo:hi], ADD)
            nc.sync.dma_start(out_rows[:, t, lo:hi], last[:, lo:hi])

        gated(a_cur, z[t], pos3_t, g2[:, 0, :], *HALVES[0])
        gated(b_cur, z[t], pos4_t, g2[:, 1, :], *HALVES[0])
        gated(a_cur, z[t], pos3_t, g2[:, 0, :], *HALVES[1])
        finish(*HALVES[0])
        gated(b_cur, z[t], pos4_t, g2[:, 1, :], *HALVES[1])
        finish(*HALVES[1])
